import numpy as np
import ml_dtypes


def mxq(x, axis, fmt="e4m3"):
    dtype, down = {"e4m3": (ml_dtypes.float8_e4m3fn, 7), "e5m2": (ml_dtypes.float8_e5m2, 14)}[fmt]
    v = np.moveaxis(np.asarray(x, np.float32).astype(ml_dtypes.bfloat16).astype(np.float64), axis, -1)
    blocks = v.reshape(v.shape[:-1] + (-1, 32))
    amax = np.abs(blocks).max(-1, keepdims=True)
    byte = np.maximum(np.where(amax > 0, np.frexp(amax)[1] - 1 + 127, 0) - down, 1)
    scale = np.exp2(byte - 127.0)
    codes = (blocks / scale).astype(np.float32).astype(dtype).astype(np.float64)
    return np.moveaxis((codes * scale).reshape(v.shape), -1, axis)


WIDE = False


def mx_kscale(k):
    if not WIDE:
        return np.ones(k)
    levels = np.array([10, -10, 5, -5, 0])
    if k % 512:
        return np.exp2(np.random.permutation(np.resize(levels, k // 32))).repeat(32)
    a = np.empty((k // 512, 16))
    for p in range(k // 512):
        a[p, :8] = np.random.permutation(np.resize(levels, 8))
        for g in range(8):
            far = levels[np.abs(levels - a[p, g]) >= 10]
            a[p, g + 8] = far[np.random.randint(len(far))]
    return np.exp2(a.ravel()).repeat(32)


BF16 = ml_dtypes.bfloat16


def bf(x):
    return np.asarray(x, np.float32).astype(BF16)


def f64(x):
    return np.asarray(x).astype(np.float64)


E2M1 = np.array([0.0, 0.5, 1.0, 1.5, 2.0, 3.0, 4.0, 6.0, -0.0, -0.5, -1.0, -1.5, -2.0, -3.0, -4.0, -6.0])


def pack_weight(w, fmt):
    k, n = w.shape
    w = f64(bf(w)).reshape(k // 32, 32, n)
    amax = np.abs(w).max(1)
    if fmt == "e4m3":
        byte = np.frexp(amax)[1] - 1 + 127 - 7
    else:
        mant, ex = np.frexp(amax / 6.0)
        byte = np.where(mant > 0.5, ex, ex - 1) + 127
    byte = np.clip(np.where(amax > 0, byte, 1), 1, 254)
    scaled = (w * np.exp2(127.0 - byte)[:, None, :]).reshape(k, n).astype(np.float32)
    by_word = np.ascontiguousarray(scaled.reshape(k // 512, 128, 4, n).transpose(0, 1, 3, 2))
    if fmt == "e4m3":
        words = by_word.astype(ml_dtypes.float8_e4m3fn).view(np.uint8)
    else:
        c = by_word.astype(ml_dtypes.float4_e2m1fn).view(np.uint8) & 0xF
        words = c[..., 0::2] | (c[..., 1::2] << 4)
    return np.ascontiguousarray(words), np.ascontiguousarray(byte.astype(np.uint8).reshape(k // 512, 16, n))


def unpack_weight(words, scales, fmt):
    g, p, n, _ = words.shape
    if fmt == "e4m3":
        vals = np.ascontiguousarray(words).view(ml_dtypes.float8_e4m3fn).astype(np.float64)
    else:
        nib = np.empty((g, p, n, 4), np.uint8)
        nib[..., 0::2] = words & 0xF
        nib[..., 1::2] = words >> 4
        vals = E2M1[nib]
    vals = vals * np.repeat(np.exp2(scales.astype(np.float64) - 127.0), 8, axis=1)[..., None]
    return vals.transpose(0, 1, 3, 2).reshape(g * 512, n)
def pack4(w):
    words, scales = pack_weight(w, "e2m1")
    return words.reshape(words.shape[0], 128, -1), scales


def unpack4(words, scales):
    return unpack_weight(words.reshape(words.shape[0], 128, -1, 2), scales, "e2m1")


N, E, O, Q, TRIPLES, PER, BITS = 1024, 4, 512, 512, 3, 3, 2
J = TRIPLES * PER
NV = BITS**J
EO = E * O


def calibrate(x, cal):
    low = np.minimum(2.0 * x, 1.0)
    high = np.maximum(2.0 * x - 1.0, 0.0)
    return cal * low + (1.0 - cal) * high


def outer3(a, b, d):
    full = a[..., :, None, None] * b[..., None, :, None] * d[..., None, None, :]
    return full.reshape(a.shape[:-1] + (-1,))


def draw0():
    ks, kt = mx_kscale(NV), mx_kscale(EO)
    inputs = {
        "x": bf(np.random.uniform(0.02, 0.98, (N, E, J))),
        "cal": bf(np.random.uniform(0.2, 0.8, (E, J))),
        "g": bf(12.0 * np.random.standard_normal((E, NV)) * ks),
        "theta": bf(0.5 * np.random.standard_normal((E, NV, O)) / ks[:, None]),
        "s": bf((1.0 + 0.1 * np.random.standard_normal(EO)) * kt),
    }
    words, scales = pack4(2.0 * np.random.standard_normal((EO, Q)) / np.sqrt(EO) / kt[:, None])
    inputs["v_words"] = words
    inputs["v_scales"] = scales
    return inputs


def core(x, cal, g, theta, s, v_words, v_scales):
    x, cal, g, theta, s = f64(x), f64(cal), f64(g), f64(theta), f64(s)
    n, e, _ = x.shape

    u = calibrate(x, cal)
    p = np.stack([1.0 - u, u], axis=-1)

    p = p.reshape(n, e, TRIPLES, PER, BITS)
    t = outer3(p[:, :, :, 0, :], p[:, :, :, 1, :], p[:, :, :, 2, :])

    w = outer3(t[:, :, 0, :], t[:, :, 1, :], t[:, :, 2, :])

    wg = w * g

    l = mxq(wg.transpose(1, 0, 2), 2, "e4m3") @ mxq(theta, 1, "e4m3")

    h = np.tanh(l)
    flat = h.transpose(1, 0, 2).reshape(n, -1)

    f = flat * s

    return mxq(f, 1, "e4m3") @ unpack4(v_words, v_scales)


def e4m3fn_bytes(y):
    return np.clip(np.asarray(y, np.float64), -448.0, 448.0).astype(np.float32).astype(ml_dtypes.float8_e4m3fn).view(np.uint8)


def e4m3fn_values(b):
    return np.asarray(b, np.uint8).view(ml_dtypes.float8_e4m3fn).astype(np.float64)


def setup_inputs():
    d = draw0()
    x0 = np.asarray(d['theta']).astype(np.float64)
    s = (np.max(np.abs(x0), axis=(0, 2), keepdims=True) / 448.0).astype(np.float32)
    out = {}
    for k, v in d.items():
        if k == 'theta':
            out['theta_bytes'] = e4m3fn_bytes(x0 / s.astype(np.float64))
            out['theta_scale'] = s
        else:
            out[k] = v
    return out


def reference(x, cal, g, theta_bytes, theta_scale, s, v_words, v_scales):
    return core(x, cal, g, e4m3fn_values(theta_bytes) * theta_scale.astype(np.float64), s, v_words, v_scales)

@@ -1,0 +1,390 @@
+from contextlib import ExitStack
+
+import concourse.mybir as mybir
+from concourse.masks import make_identity
+
+F32 = mybir.dt.float32
+BF16 = mybir.dt.bfloat16
+U32 = mybir.dt.uint32
+I32 = mybir.dt.int32
+U8 = mybir.dt.uint8
+FP8 = mybir.dt.float8_e4m3fn
+FP8X4 = mybir.dt.float8_e4m3fn_x4
+FP4X4 = mybir.dt.float4_e2m1fn_x4
+ALU = mybir.AluOpType
+ACT = mybir.ActivationFunctionType
+
+P = 128
+N, E, J, NV, O, Q = 1024, 4, 9, 512, 512, 512
+T = N // P
+TE = T * E
+TB = 4
+NB = T // TB
+UNITS = E * NB
+UN = TB * P
+
+FLOPS = 2 * N * E * NV * O + 2 * N * E * O * Q
+
+
+def tile_calibratedlatticeensemble_w4_kernel(tc, x, cal, g, theta_bytes, theta_scale, s, v_words, v_scales, out):
+    nc = tc.nc
+    with ExitStack() as ctx:
+        const = ctx.enter_context(tc.tile_pool(name="const", bufs=1))
+        head = ctx.enter_context(tc.tile_pool(name="head", bufs=1))
+        work = ctx.enter_context(tc.tile_pool(name="work", bufs=3))
+        ps_a = ctx.enter_context(tc.psum_pool(name="ps_a", bufs=5))
+        ps_l = ctx.enter_context(tc.psum_pool(name="ps_l", bufs=3))
+        ctx.enter_context(tc.manual_schedule())
+
+        x_sb = head.tile([P, T * E * J], BF16)
+        nc.sync.dma_start(out=x_sb[:], in_=x.rearrange("(p t) e j -> p (t e j)", t=T))
+        cal_sb = head.tile([P, E * J], BF16)
+        nc.sync.dma_start(out=cal_sb[:], in_=cal.rearrange("e j -> (e j)").partition_broadcast(P))
+        tsc = const.tile([P, 4], F32)
+        nc.sync.dma_start(out=tsc[:], in_=theta_scale.rearrange("o (p j) z -> p (o j z)", j=4))
+        tb = [const.tile([P, 4 * O], U8, name=f"tb{e}") for e in range(E)]
+
+        def load_theta(e):
+            nc.sync.dma_start(out=tb[e][:], in_=theta_bytes[e].rearrange("(p j) o -> p (j o)", j=4))
+
+        load_theta(0)
+        g_sb = const.tile([P, E * NV], BF16)
+        nc.sync.dma_start(out=g_sb[:], in_=g.rearrange("e i -> (e i)").partition_broadcast(P))
+        s_bf = head.tile([P, E, 4], BF16)
+        nc.sync.dma_start(out=s_bf[:], in_=s.rearrange("(e p t) -> p e t", p=P, t=4))
+        for e in range(1, E):
+            load_theta(e)
+        vs = const.tile([P, E, Q], U8, align_bytes=64)
+        vw = const.tile([P, E, 2 * Q], U8, align_bytes=64)
+        nc.gpsimd.memset(vs[:].rearrange("p g n -> p (g n)").bitcast(I32), 0)
+        nc.sync.dma_start(out=vw[:], in_=v_words.rearrange("g p b -> p g b"))
+        for q in range(4):
+            nc.sync.dma_start(
+                out=vs[32 * q : 32 * q + 4].bitcast(I32),
+                in_=v_scales[:, 4 * q : 4 * q + 4, :].rearrange("g r n -> r g n").bitcast(I32),
+            )
+
+        warm = head.tile([P, 1], F32)
+        nc.vector.memset(warm[:], 0.0)
+        warm2 = head.tile([P, 1], F32)
+        nc.scalar.activation(out=warm2[:], in_=warm[:], func=ACT.Tanh)
+        rn = head.tile([P, T, P], BF16)
+        nc.vector.memset(rn[:], 0.0)
+
+        ident = const.tile([P, P], F32)
+        make_identity(nc, ident[:])
+        ident_b = const.tile([P, P], BF16)
+        nc.gpsimd.tensor_copy(out=ident_b[:], in_=ident[:])
+        pick2 = head.tile([P, 16], F32)
+        nc.gpsimd.tensor_tensor(out=pick2[:], in0=ident[:, 0:16], in1=ident[:, 16:32], op=ALU.add)
+        pick = head.tile([P, 16], F32)
+        nc.gpsimd.tensor_tensor(out=pick[:], in0=pick2[:], in1=ident[:, 32:48], op=ALU.add)
+        gl = const.tile([P, E, 3, P], BF16)
+        g_view = g_sb[:].rearrange("p (e m t) -> p e t m", e=E, t=4)
+
+        def make_gl(e):
+            nc.gpsimd.tensor_tensor(
+                out=gl[:, e],
+                in0=g_view[:, e, 0:3, :],
+                in1=pick[:, 4 * e : 4 * e + 3].unsqueeze(2).to_broadcast([P, 3, P]),
+                op=ALU.mult,
+            )
+
+        tw = {}
+        tg = {}
+        thc = [const.tile([P, O], U32, name=f"thc{e}", align_bytes=64) for e in range(E)]
+        ths = [const.tile([P, O], U8, name=f"ths{e}", align_bytes=64) for e in range(E)]
+
+        def theta_widen(e):
+            tw[e] = work.tile([P, 4, O], BF16, name="tw", tag="tw", bufs=2)
+            for j in range(4):
+                nc.scalar.activation(
+                    out=tw[e][:, j, :],
+                    in_=tb[e][:, j * O : (j + 1) * O].bitcast(FP8),
+                    func=ACT.Copy,
+                    scale=tsc[:, j : j + 1],
+                )
+
+        def theta_interleave(e):
+            tg[e] = work.tile([P, 4 * O], BF16, name="tg", tag="tg", bufs=2, align_bytes=64)
+            nc.scalar.copy(
+                out=tg[e][:].rearrange("p (t m j) -> p m t j", t=4, j=4),
+                in_=tw[e][:].rearrange("p j (m t) -> p m t j", t=4),
+            )
+
+        def theta_quantize(e):
+            nc.vector.quantize_mx(out=thc[e][:].bitcast(FP8X4), scales=ths[e][:], in_=tg[e][:])
+
+        pp = head.tile([P, TE, J, 2], F32)
+        low = head.tile([P, TE * J], F32)
+        high = head.tile([P, TE * J], F32)
+        dd = head.tile([P, TE * J], F32)
+        mm = head.tile([P, TE * J], F32)
+        pv = pp[:].rearrange("p a j b -> p (a j) b")
+        theta_widen(0)
+        theta_interleave(0)
+        make_gl(0)
+        nc.vector.tensor_scalar(out=low[:], in0=x_sb[:], scalar1=2.0, scalar2=1.0, op0=ALU.mult, op1=ALU.min)
+        nc.vector.tensor_tensor(out=dd[:], in0=low[:], in1=x_sb[:], op=ALU.subtract)
+        nc.vector.scalar_tensor_tensor(out=high[:], in0=x_sb[:], scalar=2.0, in1=low[:], op0=ALU.mult, op1=ALU.subtract)
+        nc.vector.scalar_tensor_tensor(
+            out=mm[:].rearrange("p (t c) -> p t c", t=T),
+            in0=dd[:].rearrange("p (t c) -> p t c", t=T),
+            scalar=2.0,
+            in1=cal_sb[:].unsqueeze(1).to_broadcast([P, T, E * J]),
+            op0=ALU.mult,
+            op1=ALU.mult,
+        )
+        nc.vector.tensor_tensor(out=pv[:, :, 1], in0=mm[:], in1=high[:], op=ALU.add)
+        nc.vector.tensor_scalar(out=pv[:, :, 0], in0=pv[:, :, 1], scalar1=-1.0, scalar2=1.0, op0=ALU.mult, op1=ALU.add)
+
+        def outer(dst, a, b, na, nb):
+            nc.vector.tensor_tensor(
+                out=dst.rearrange("p a (b c) -> p a b c", c=nb),
+                in0=a.unsqueeze(3).to_broadcast([P, TE, na, nb]),
+                in1=b.unsqueeze(2).to_broadcast([P, TE, na, nb]),
+                op=ALU.mult,
+            )
+
+        q78 = head.tile([P, TE, 4], F32)
+        q01 = head.tile([P, TE, 4], F32)
+        q23 = head.tile([P, TE, 4], F32)
+        q45 = head.tile([P, TE, 4], F32)
+        q0123 = head.tile([P, TE, 16], F32)
+        q456 = head.tile([P, TE, 8], F32)
+        w2 = q78[:].rearrange("p (t e) b -> p t (e b)", e=E)
+        r1 = head.tile([P, T, 16], F32)
+        r2 = head.tile([P, T, 16], F32)
+        outer(q78[:], pp[:, :, 7, :], pp[:, :, 8, :], 2, 2)
+        outer(q01[:], pp[:, :, 0, :], pp[:, :, 1, :], 2, 2)
+        nc.vector.tensor_copy(out=rn[:, :, 0:16], in_=w2)
+        outer(q23[:], pp[:, :, 2, :], pp[:, :, 3, :], 2, 2)
+        nc.vector.tensor_tensor(out=r1[:], in0=w2, in1=rn[:, :, 0:16], op=ALU.subtract)
+        outer(q45[:], pp[:, :, 4, :], pp[:, :, 5, :], 2, 2)
+        nc.vector.tensor_copy(out=rn[:, :, 16:32], in_=r1[:])
+        outer(q0123[:], q01[:], q23[:], 4, 4)
+        nc.vector.tensor_tensor(out=r2[:], in0=r1[:], in1=rn[:, :, 16:32], op=ALU.subtract)
+        outer(q456[:], q45[:], pp[:, :, 6, :], 4, 2)
+        nc.vector.tensor_copy(out=rn[:, :, 32:48], in_=r2[:])
+
+        q0123_v = q0123[:].rearrange("p (t e) b -> p t e b", e=E)
+        q456_v = q456[:].rearrange("p (t e) b -> p t e b", e=E)
+        q78_v = q78[:].rearrange("p (t e) b -> p t e b", e=E)
+        w7 = {}
+        y3 = {}
+        fs = {}
+        gw = {}
+        ft = {}
+        wg = {}
+        wgc = {}
+        wgs = {}
+        lt = {}
+        h = {}
+        f = {}
+        fc = {}
+        fsc = {}
+        acc = {}
+
+        def make_w7(i, eng):
+            e, b = i // NB, i % NB
+            w7[i] = work.tile([P, TB, P], F32, name="w7", tag="w7")
+            eng.tensor_tensor(
+                out=w7[i][:].rearrange("p t (a b) -> p t a b", b=8),
+                in0=q0123_v[:, TB * b : TB * b + TB, e, :].unsqueeze(3).to_broadcast([P, TB, 16, 8]),
+                in1=q456_v[:, TB * b : TB * b + TB, e, :].unsqueeze(2).to_broadcast([P, TB, 16, 8]),
+                op=ALU.mult,
+            )
+
+        def make_y3(i):
+            e, b = i // NB, i % NB
+            y3[i] = work.tile([P, TB, P], F32, name="y3", tag="y3")
+            nc.gpsimd.tensor_tensor(
+                out=y3[i][:],
+                in0=g_view[:, e, 3, :].unsqueeze(1).to_broadcast([P, TB, P]),
+                in1=q78_v[:, TB * b : TB * b + TB, e, 3:4].to_broadcast([P, TB, P]),
+                op=ALU.mult,
+            )
+
+        def transpose_w7(i):
+            ft[i] = ps_a.tile([P, TB, P], F32, name="ft", tag="bank")
+            for k in range(TB):
+                nc.tensor.transpose(ft[i][:, k, :], w7[i][:, k, :], ident[:])
+
+        def copy_w7(i):
+            fs[i] = work.tile([P, TB, P], F32, name="fs", tag="fs")
+            nc.scalar.copy(out=fs[i][:], in_=ft[i][:])
+
+        def transpose_y3(i):
+            for k in range(TB):
+                gw[i, k] = ps_a.tile([P, 4, P], F32, name="gw", tag="bank")
+                nc.tensor.transpose(gw[i, k][:, 3, :], y3[i][:, k, :], ident[:])
+
+        def multiply_gw(i):
+            e, b = i // NB, i % NB
+            for k in range(TB):
+                t0 = (TB * b + k) * P
+                for t in range(3):
+                    nc.tensor.matmul(gw[i, k][:, t, :], lhsT=gl[:, e, t, :], rhs=rt[:, t0 : t0 + P], start=True, stop=True)
+
+        def make_wg(i, k):
+            if k == 0:
+                wg[i] = work.tile([P, TB, P, 4], BF16, name="wg", tag="wg", align_bytes=64)
+            nc.vector.tensor_tensor(
+                out=wg[i][:, k],
+                in0=gw[i, k][:].rearrange("p t n -> p n t"),
+                in1=fs[i][:, k, :].unsqueeze(2).to_broadcast([P, P, 4]),
+                op=ALU.mult,
+            )
+
+        def quantize_wg(i):
+            wgc[i] = work.tile([P, UN], U32, name="wgc", tag="wgc", align_bytes=64)
+            wgs[i] = work.tile([P, UN], U8, name="wgs", tag="wgs", align_bytes=64)
+            nc.vector.quantize_mx(
+                out=wgc[i][:].bitcast(FP8X4), scales=wgs[i][:], in_=wg[i][:].rearrange("p a n t -> p (a n t)")
+            )
+
+        def stage1(i, k):
+            e = i // NB
+            lt[i, k] = ps_l.tile([P, 4, P], F32, name="lt", tag="bank")
+            n0 = k * P
+            for t in range(4):
+                nc.tensor.matmul_mx(
+                    out=lt[i, k][:, t, :],
+                    lhsT=thc[e][:, t * P : t * P + P].bitcast(FP8X4),
+                    lhsT_scale=ths[e][:, t * P : t * P + P],
+                    rhs=wgc[i][:, n0 : n0 + P].bitcast(FP8X4),
+                    rhs_scale=wgs[i][:, n0 : n0 + P],
+                    start=True,
+                    stop=True,
+                )
+
+        def tanh(i, k):
+            if k == 0:
+                h[i] = work.tile([P, TB, P, 4], F32, name="h", tag="h")
+            nc.scalar.activation(out=h[i][:, k], in_=lt[i, k][:].rearrange("p t n -> p n t"), func=ACT.Tanh)
+
+        def make_f(i, k, n):
+            e = i // NB
+            if k == 0:
+                f[i] = work.tile([P, UN, 4], BF16, name="f", tag="f", align_bytes=64)
+            nc.vector.tensor_tensor(
+                out=f[i][:, k * P : (k + n) * P, :],
+                in0=h[i][:, k : k + n].rearrange("p a n t -> p (a n) t"),
+                in1=s_sb[:, e, :].unsqueeze(1).to_broadcast([P, n * P, 4]),
+                op=ALU.mult,
+            )
+
+        def quantize_f(i, k, n):
+            if k == 0:
+                fc[i] = const.tile([P, UN], U32, name=f"fc{i}", align_bytes=64)
+                fsc[i] = const.tile([P, UN], U8, name=f"fsc{i}", align_bytes=64)
+            c = slice(k * P, (k + n) * P)
+            nc.vector.quantize_mx(
+                out=fc[i][:, c].bitcast(FP8X4), scales=fsc[i][:, c], in_=f[i][:, c, :].rearrange("p n t -> p (n t)")
+            )
+
+        def stage2(tile, members):
+            b, k = tile // TB, tile % TB
+            c = slice(k * P, k * P + P)
+            for e in members:
+                i = e * NB + b
+                nc.tensor.matmul_mx(
+                    out=acc[tile][:],
+                    lhsT=fc[i][:, c].bitcast(FP8X4),
+                    lhsT_scale=fsc[i][:, c],
+                    rhs=vw[:, e, :].bitcast(FP4X4),
+                    rhs_scale=vs[:, e, :],
+                    start=(e == 0),
+                    stop=(e == E - 1),
+                )
+
+        out_v = out.rearrange("(p t) q -> t p q", t=T)
+
+        def store(tile, on_vector):
+            o = work.tile([P, Q], F32, name="o", tag="o")
+            if on_vector:
+                nc.vector.tensor_copy(out=o[:], in_=acc[tile][:])
+            else:
+                nc.scalar.copy(out=o[:], in_=acc[tile][:])
+            nc.sync.dma_start(out=out_v[tile], in_=o[:])
+
+        make_w7(0, nc.vector)
+        make_y3(0)
+        make_w7(1, nc.gpsimd)
+        make_y3(1)
+        make_gl(1)
+        make_w7(2, nc.gpsimd)
+
+        rt = const.tile([P, N], BF16)
+        for half in range(2):
+            rt_ps = ps_a.tile([P, TB, P], BF16, name="rt_ps", tag="bank")
+            for k in range(TB):
+                nc.tensor.transpose(rt_ps[:, k, :], rn[:, TB * half + k, :], ident_b[:])
+            nc.scalar.copy(out=rt[:, half * UN : half * UN + UN], in_=rt_ps[:].rearrange("p a n -> p (a n)"))
+        transpose_w7(0)
+        copy_w7(0)
+        s_sb = const.tile([P, E, 4], F32)
+        nc.gpsimd.tensor_copy(out=s_sb[:], in_=s_bf[:])
+        theta_quantize(0)
+        transpose_y3(0)
+        multiply_gw(0)
+        transpose_w7(1)
+        copy_w7(1)
+
+        for i in range(UNITS):
+            make_wg(i, 0)
+            make_wg(i, 1)
+            if i >= 2:
+                quantize_f(i - 2, 0, TB)
+            if i % NB == 0 and i > 0:
+                theta_quantize(i // NB)
+            make_wg(i, 2)
+            make_wg(i, 3)
+            if i + 3 < UNITS:
+                make_w7(i + 3, nc.gpsimd)
+            if i + 2 < UNITS:
+                make_y3(i + 2)
+            if i < 2:
+                make_gl(i + 2)
+            if i + 1 < UNITS:
+                transpose_y3(i + 1)
+            if i + 2 < UNITS:
+                transpose_w7(i + 2)
+            if i + 1 < UNITS:
+                multiply_gw(i + 1)
+            if i % NB == 0 and i // NB + 1 < E:
+                theta_widen(i // NB + 1)
+            if i % NB == 1 and i // NB + 1 < E:
+                theta_interleave(i // NB + 1)
+            if i + 2 < UNITS:
+                copy_w7(i + 2)
+            if i >= 1:
+                make_f(i - 1, 0, 2)
+            quantize_wg(i)
+            if i >= 1:
+                make_f(i - 1, 2, 2)
+            if i == UNITS - 1:
+                for tile in range(TB):
+                    acc[tile] = ps_a.tile([P, Q], F32, name="acc", tag="bank")
+                    stage2(tile, range(E - 1))
+            for k in range(TB):
+                stage1(i, k)
+                tanh(i, k)
+
+        last = UNITS - 1
+        acc[TB] = ps_a.tile([P, Q], F32, name="acc", tag="bank")
+        stage2(TB, range(E - 1))
+        quantize_f(last - 1, 0, TB)
+        for tile in range(TB):
+            stage2(tile, [E - 1])
+            store(tile, False)
+        for tile in range(TB + 1, T):
+            acc[tile] = ps_l.tile([P, Q], F32, name="acc2", tag="bank")
+            stage2(tile, range(E - 1))
+        for k in range(TB):
+            make_f(last, k, 1)
+            if k % 2 == 1:
+                quantize_f(last, k - 1, 2)
+        for tile in range(TB, T):
+            stage2(tile, [E - 1])
+            store(tile, tile == T - 2)

@@ -22,6 +22,9 @@ TB = 4
 NB = T // TB
 UNITS = E * NB
 UN = TB * P
+Y3 = "s"
+FG = False
+LG = True
 
 FLOPS = 2 * N * E * NV * O + 2 * N * E * O * Q
 
@@ -83,12 +86,12 @@ def tile_calibratedlatticeensemble_w4_kernel(tc, x, cal, g, theta_bytes, theta_s
         g_view = g_sb[:].rearrange("p (e m t) -> p e t m", e=E, t=4)
 
         def make_gl(e):
-            nc.gpsimd.tensor_tensor(
-                out=gl[:, e],
-                in0=g_view[:, e, 0:3, :],
-                in1=pick[:, 4 * e : 4 * e + 3].unsqueeze(2).to_broadcast([P, 3, P]),
-                op=ALU.mult,
-            )
+            for t in range(3):
+                c = pick[:, 4 * e + t : 4 * e + t + 1]
+                if LG and e > 0:
+                    nc.gpsimd.tensor_scalar(out=gl[:, e, t, :], in0=g_view[:, e, t, :], scalar1=c, scalar2=0.0, op0=ALU.mult, op1=ALU.add)
+                else:
+                    nc.scalar.activation(out=gl[:, e, t, :], in_=g_view[:, e, t, :], func=ACT.Copy, scale=c)
 
         tw = {}
         tg = {}
@@ -116,59 +119,62 @@ def tile_calibratedlatticeensemble_w4_kernel(tc, x, cal, g, theta_bytes, theta_s
             nc.vector.quantize_mx(out=thc[e][:].bitcast(FP8X4), scales=ths[e][:], in_=tg[e][:])
 
         pp = head.tile([P, TE, J, 2], F32)
-        low = head.tile([P, TE * J], F32)
+        dist = head.tile([P, TE * J], F32)
         high = head.tile([P, TE * J], F32)
-        dd = head.tile([P, TE * J], F32)
-        mm = head.tile([P, TE * J], F32)
+        bend = head.tile([P, TE * J], F32)
         pv = pp[:].rearrange("p a j b -> p (a j) b")
-        theta_widen(0)
-        theta_interleave(0)
-        make_gl(0)
-        nc.vector.tensor_scalar(out=low[:], in0=x_sb[:], scalar1=2.0, scalar2=1.0, op0=ALU.mult, op1=ALU.min)
-        nc.vector.tensor_tensor(out=dd[:], in0=low[:], in1=x_sb[:], op=ALU.subtract)
-        nc.vector.scalar_tensor_tensor(out=high[:], in0=x_sb[:], scalar=2.0, in1=low[:], op0=ALU.mult, op1=ALU.subtract)
-        nc.vector.scalar_tensor_tensor(
-            out=mm[:].rearrange("p (t c) -> p t c", t=T),
-            in0=dd[:].rearrange("p (t c) -> p t c", t=T),
-            scalar=2.0,
-            in1=cal_sb[:].unsqueeze(1).to_broadcast([P, T, E * J]),
-            op0=ALU.mult,
-            op1=ALU.mult,
-        )
-        nc.vector.tensor_tensor(out=pv[:, :, 1], in0=mm[:], in1=high[:], op=ALU.add)
-        nc.vector.tensor_scalar(out=pv[:, :, 0], in0=pv[:, :, 1], scalar1=-1.0, scalar2=1.0, op0=ALU.mult, op1=ALU.add)
-
-        def outer(dst, a, b, na, nb):
-            nc.vector.tensor_tensor(
-                out=dst.rearrange("p a (b c) -> p a b c", c=nb),
-                in0=a.unsqueeze(3).to_broadcast([P, TE, na, nb]),
-                in1=b.unsqueeze(2).to_broadcast([P, TE, na, nb]),
-                op=ALU.mult,
-            )
-
         q78 = head.tile([P, TE, 4], F32)
         q01 = head.tile([P, TE, 4], F32)
         q23 = head.tile([P, TE, 4], F32)
         q45 = head.tile([P, TE, 4], F32)
         q0123 = head.tile([P, TE, 16], F32)
-        q456 = head.tile([P, TE, 8], F32)
+        qg = head.tile([P, TE, 8], F32)
         w2 = q78[:].rearrange("p (t e) b -> p t (e b)", e=E)
         r1 = head.tile([P, T, 16], F32)
-        r2 = head.tile([P, T, 16], F32)
-        outer(q78[:], pp[:, :, 7, :], pp[:, :, 8, :], 2, 2)
-        outer(q01[:], pp[:, :, 0, :], pp[:, :, 1, :], 2, 2)
-        nc.vector.tensor_copy(out=rn[:, :, 0:16], in_=w2)
-        outer(q23[:], pp[:, :, 2, :], pp[:, :, 3, :], 2, 2)
-        nc.vector.tensor_tensor(out=r1[:], in0=w2, in1=rn[:, :, 0:16], op=ALU.subtract)
-        outer(q45[:], pp[:, :, 4, :], pp[:, :, 5, :], 2, 2)
-        nc.vector.tensor_copy(out=rn[:, :, 16:32], in_=r1[:])
-        outer(q0123[:], q01[:], q23[:], 4, 4)
-        nc.vector.tensor_tensor(out=r2[:], in0=r1[:], in1=rn[:, :, 16:32], op=ALU.subtract)
-        outer(q456[:], q45[:], pp[:, :, 6, :], 4, 2)
-        nc.vector.tensor_copy(out=rn[:, :, 32:48], in_=r2[:])
+        minus1 = head.tile([P, 1], F32)
+        nc.vector.memset(minus1[:], -1.0)
+        nc.scalar.activation(out=dist[:], in_=x_sb[:], func=ACT.Abs, scale=2.0, bias=minus1[:])
+        nc.scalar.activation(out=high[:], in_=x_sb[:], func=ACT.Relu, scale=2.0, bias=minus1[:])
+
+        def outer(b, dst, u, v, na, nv):
+            r = slice(b * TB * E, (b + 1) * TB * E)
+            n = TB * E
+            nc.vector.tensor_tensor(
+                out=dst[:, r, 0 : na * nv].rearrange("p a (b c) -> p a b c", c=nv),
+                in0=u[:, r, :].unsqueeze(3).to_broadcast([P, n, na, nv]),
+                in1=v[:, r, :].unsqueeze(2).to_broadcast([P, n, na, nv]),
+                op=ALU.mult,
+            )
+
+        def prepare(b):
+            c = slice(b * TB * E * J, (b + 1) * TB * E * J)
+            tt = slice(b * TB, (b + 1) * TB)
+            V = nc.vector
+            return [
+                lambda: V.scalar_tensor_tensor(
+                    out=bend[:, c].rearrange("p (t c) -> p t c", t=TB),
+                    in0=dist[:, c].rearrange("p (t c) -> p t c", t=TB),
+                    scalar=-1.0,
+                    in1=cal_sb[:].unsqueeze(1).to_broadcast([P, TB, E * J]),
+                    op0=ALU.add,
+                    op1=ALU.mult,
+                ),
+                lambda: V.tensor_tensor(out=pv[:, c, 1], in0=high[:, c], in1=bend[:, c], op=ALU.subtract),
+                lambda: V.tensor_scalar(out=pv[:, c, 0], in0=pv[:, c, 1], scalar1=-1.0, scalar2=1.0, op0=ALU.mult, op1=ALU.add),
+                lambda: outer(b, q78, pp[:, :, 7, :], pp[:, :, 8, :], 2, 2),
+                lambda: outer(b, q01, pp[:, :, 0, :], pp[:, :, 1, :], 2, 2),
+                lambda: outer(b, q23, pp[:, :, 2, :], pp[:, :, 3, :], 2, 2),
+                lambda: V.tensor_copy(out=rn[:, tt, 0:16], in_=w2[:, tt]),
+                lambda: outer(b, q45, pp[:, :, 4, :], pp[:, :, 5, :], 2, 2),
+                lambda: V.tensor_tensor(out=rn[:, tt, 16:32], in0=w2[:, tt], in1=rn[:, tt, 0:16], op=ALU.subtract),
+                lambda: V.tensor_tensor(out=r1[:, tt], in0=w2[:, tt], in1=rn[:, tt, 0:16], op=ALU.subtract),
+                lambda: outer(b, q0123, q01[:], q23[:], 4, 4),
+                lambda: outer(b, qg, q45[:], pp[:, :, 6, :], 4, 2),
+                lambda: V.tensor_tensor(out=rn[:, tt, 32:48], in0=r1[:, tt], in1=rn[:, tt, 16:32], op=ALU.subtract),
+            ]
 
         q0123_v = q0123[:].rearrange("p (t e) b -> p t e b", e=E)
-        q456_v = q456[:].rearrange("p (t e) b -> p t e b", e=E)
+        qg_v = qg[:].rearrange("p (t e) b -> p t e b", e=E)
         q78_v = q78[:].rearrange("p (t e) b -> p t e b", e=E)
         w7 = {}
         y3 = {}
@@ -185,25 +191,47 @@ def tile_calibratedlatticeensemble_w4_kernel(tc, x, cal, g, theta_bytes, theta_s
         fsc = {}
         acc = {}
 
-        def make_w7(i, eng):
+        gate = {}
+
+        def make_gate(i):
+            e, b = i // NB, i % NB
+            gate[i] = work.tile([P, TB, 8], F32, name="gate", tag="gate")
+            nc.vector.tensor_copy(out=gate[i][:], in_=qg_v[:, TB * b : TB * b + TB, e, :])
+
+        def make_w7(i, eng, src):
             e, b = i // NB, i % NB
             w7[i] = work.tile([P, TB, P], F32, name="w7", tag="w7")
             eng.tensor_tensor(
                 out=w7[i][:].rearrange("p t (a b) -> p t a b", b=8),
                 in0=q0123_v[:, TB * b : TB * b + TB, e, :].unsqueeze(3).to_broadcast([P, TB, 16, 8]),
-                in1=q456_v[:, TB * b : TB * b + TB, e, :].unsqueeze(2).to_broadcast([P, TB, 16, 8]),
+                in1=src.unsqueeze(2).to_broadcast([P, TB, 16, 8]),
                 op=ALU.mult,
             )
 
-        def make_y3(i):
+        def make_y3(i, how):
             e, b = i // NB, i % NB
             y3[i] = work.tile([P, TB, P], F32, name="y3", tag="y3")
-            nc.gpsimd.tensor_tensor(
-                out=y3[i][:],
-                in0=g_view[:, e, 3, :].unsqueeze(1).to_broadcast([P, TB, P]),
-                in1=q78_v[:, TB * b : TB * b + TB, e, 3:4].to_broadcast([P, TB, P]),
-                op=ALU.mult,
-            )
+            if how == "v":
+                for k in range(TB):
+                    a = (TB * b + k) * E + e
+                    nc.vector.tensor_scalar(out=y3[i][:, k, :], in0=g_view[:, e, 3, :], scalar1=q78[:, a, 3:4], scalar2=None, op0=ALU.mult)
+            elif how == "s":
+                for k in range(TB):
+                    a = (TB * b + k) * E + e
+                    nc.scalar.activation(out=y3[i][:, k, :], in_=g_view[:, e, 3, :], func=ACT.Copy, scale=q78[:, a, 3:4])
+            else:
+                nc.gpsimd.tensor_tensor(
+                    out=y3[i][:],
+                    in0=g_view[:, e, 3, :].unsqueeze(1).to_broadcast([P, TB, P]),
+                    in1=gate[i][:, :, 8:9].to_broadcast([P, TB, P]),
+                    op=ALU.mult,
+                )
+
+        def half_rt(half):
+            rt_ps = ps_a.tile([P, TB, P], BF16, name="rt_ps", tag="bank")
+            for k in range(TB):
+                nc.tensor.transpose(rt_ps[:, k, :], rn[:, TB * half + k, :], ident_b[:])
+            nc.scalar.copy(out=rt[:, half * UN : half * UN + UN], in_=rt_ps[:].rearrange("p a n -> p (a n)"))
 
         def transpose_w7(i):
             ft[i] = ps_a.tile([P, TB, P], F32, name="ft", tag="bank")
@@ -263,11 +291,11 @@ def tile_calibratedlatticeensemble_w4_kernel(tc, x, cal, g, theta_bytes, theta_s
                 h[i] = work.tile([P, TB, P, 4], F32, name="h", tag="h")
             nc.scalar.activation(out=h[i][:, k], in_=lt[i, k][:].rearrange("p t n -> p n t"), func=ACT.Tanh)
 
-        def make_f(i, k, n):
+        def make_f(i, k, n, eng=nc.vector):
             e = i // NB
             if k == 0:
                 f[i] = work.tile([P, UN, 4], BF16, name="f", tag="f", align_bytes=64)
-            nc.vector.tensor_tensor(
+            eng.tensor_tensor(
                 out=f[i][:, k * P : (k + n) * P, :],
                 in0=h[i][:, k : k + n].rearrange("p a n t -> p (a n) t"),
                 in1=s_sb[:, e, :].unsqueeze(1).to_broadcast([P, n * P, 4]),
@@ -301,68 +329,76 @@ def tile_calibratedlatticeensemble_w4_kernel(tc, x, cal, g, theta_bytes, theta_s
         out_v = out.rearrange("(p t) q -> t p q", t=T)
 
         def store(tile, on_vector):
-            o = work.tile([P, Q], F32, name="o", tag="o")
+            o = work.tile([P, Q], F32, name="o", tag="o", bufs=8)
             if on_vector:
                 nc.vector.tensor_copy(out=o[:], in_=acc[tile][:])
             else:
                 nc.scalar.copy(out=o[:], in_=acc[tile][:])
             nc.sync.dma_start(out=out_v[tile], in_=o[:])
 
-        make_w7(0, nc.vector)
-        make_y3(0)
-        make_w7(1, nc.gpsimd)
-        make_y3(1)
-        make_gl(1)
-        make_w7(2, nc.gpsimd)
-
         rt = const.tile([P, N], BF16)
-        for half in range(2):
-            rt_ps = ps_a.tile([P, TB, P], BF16, name="rt_ps", tag="bank")
-            for k in range(TB):
-                nc.tensor.transpose(rt_ps[:, k, :], rn[:, TB * half + k, :], ident_b[:])
-            nc.scalar.copy(out=rt[:, half * UN : half * UN + UN], in_=rt_ps[:].rearrange("p a n -> p (a n)"))
-        transpose_w7(0)
-        copy_w7(0)
         s_sb = const.tile([P, E, 4], F32)
         nc.gpsimd.tensor_copy(out=s_sb[:], in_=s_bf[:])
-        theta_quantize(0)
+        theta_widen(0)
+        make_gl(0)
+        for step in prepare(0):
+            step()
+        make_w7(0, nc.vector, qg_v[:, 0:TB, 0, 0:8])
+        half_rt(0)
+        make_y3(0, "s")
+        transpose_w7(0)
+        copy_w7(0)
         transpose_y3(0)
         multiply_gw(0)
+        rest = prepare(1)
+        weave = [6, 9, 11, 13]
+        for k in range(TB):
+            for n in range(weave[k - 1] if k else 0, weave[k]):
+                rest[n]()
+            make_wg(0, k)
+        theta_interleave(0)
+        half_rt(1)
+        make_y3(1, "s")
+        make_w7(1, nc.vector, qg_v[:, TB:T, 0, 0:8])
         transpose_w7(1)
         copy_w7(1)
+        theta_quantize(0)
 
         for i in range(UNITS):
-            make_wg(i, 0)
-            make_wg(i, 1)
+            if i + 2 < UNITS:
+                make_gate(i + 2)
+                make_w7(i + 2, nc.gpsimd, gate[i + 2][:, :, 0:8])
+            if i % NB == 0 and i // NB + 1 < E and LG:
+                make_gl(i // NB + 1)
+            if FG and i >= 2:
+                make_f(i - 2, 3, 1, nc.gpsimd)
+            if i > 0:
+                for k in range(TB):
+                    make_wg(i, k)
             if i >= 2:
                 quantize_f(i - 2, 0, TB)
             if i % NB == 0 and i > 0:
                 theta_quantize(i // NB)
-            make_wg(i, 2)
-            make_wg(i, 3)
-            if i + 3 < UNITS:
-                make_w7(i + 3, nc.gpsimd)
             if i + 2 < UNITS:
-                make_y3(i + 2)
-            if i < 2:
-                make_gl(i + 2)
-            if i + 1 < UNITS:
-                transpose_y3(i + 1)
-            if i + 2 < UNITS:
-                transpose_w7(i + 2)
-            if i + 1 < UNITS:
-                multiply_gw(i + 1)
+                make_y3(i + 2, Y3)
             if i % NB == 0 and i // NB + 1 < E:
+                if not LG:
+                    make_gl(i // NB + 1)
                 theta_widen(i // NB + 1)
             if i % NB == 1 and i // NB + 1 < E:
                 theta_interleave(i // NB + 1)
-            if i + 2 < UNITS:
-                copy_w7(i + 2)
-            if i >= 1:
-                make_f(i - 1, 0, 2)
-            quantize_wg(i)
-            if i >= 1:
-                make_f(i - 1, 2, 2)
+            if i + 1 < UNITS:
+                transpose_y3(i + 1)
+                multiply_gw(i + 1)
+            if i == UNITS - 1:
+                quantize_wg(i)
+                make_f(i - 1, 0, 4)
+            else:
+                if i >= 1:
+                    make_f(i - 1, 0, 2)
+                quantize_wg(i)
+                if i >= 1:
+                    make_f(i - 1, 2, 1 if FG else 2)
             if i == UNITS - 1:
                 for tile in range(TB):
                     acc[tile] = ps_a.tile([P, Q], F32, name="acc", tag="bank")
@@ -370,21 +406,24 @@ def tile_calibratedlatticeensemble_w4_kernel(tc, x, cal, g, theta_bytes, theta_s
             for k in range(TB):
                 stage1(i, k)
                 tanh(i, k)
+            if i + 2 < UNITS:
+                transpose_w7(i + 2)
+                copy_w7(i + 2)
 
         last = UNITS - 1
         acc[TB] = ps_a.tile([P, Q], F32, name="acc", tag="bank")
         stage2(TB, range(E - 1))
         quantize_f(last - 1, 0, TB)
-        for tile in range(TB):
-            stage2(tile, [E - 1])
-            store(tile, False)
         for tile in range(TB + 1, T):
             acc[tile] = ps_l.tile([P, Q], F32, name="acc2", tag="bank")
             stage2(tile, range(E - 1))
+        for tile in range(TB):
+            stage2(tile, [E - 1])
+            store(tile, False)
         for k in range(TB):
             make_f(last, k, 1)
             if k % 2 == 1:
                 quantize_f(last, k - 1, 2)
         for tile in range(TB, T):
             stage2(tile, [E - 1])
-            store(tile, tile == T - 2)
+            store(tile, tile >= T - 2)

from contextlib import ExitStack

import concourse.mybir as mybir
from concourse.masks import make_identity

F32 = mybir.dt.float32
BF16 = mybir.dt.bfloat16
U32 = mybir.dt.uint32
I32 = mybir.dt.int32
U8 = mybir.dt.uint8
FP8 = mybir.dt.float8_e4m3fn
FP8X4 = mybir.dt.float8_e4m3fn_x4
FP4X4 = mybir.dt.float4_e2m1fn_x4
ALU = mybir.AluOpType
ACT = mybir.ActivationFunctionType

P = 128
N, E, J, NV, O, Q = 1024, 4, 9, 512, 512, 512
T = N // P
TE = T * E
TB = 4
NB = T // TB
UNITS = E * NB
UN = TB * P
Y3 = "s"
FG = False
LG = True

FLOPS = 2 * N * E * NV * O + 2 * N * E * O * Q


def tile_calibratedlatticeensemble_w4_kernel(tc, x, cal, g, theta_bytes, theta_scale, s, v_words, v_scales, out):
    nc = tc.nc
    with ExitStack() as ctx:
        const = ctx.enter_context(tc.tile_pool(name="const", bufs=1))
        head = ctx.enter_context(tc.tile_pool(name="head", bufs=1))
        work = ctx.enter_context(tc.tile_pool(name="work", bufs=3))
        ps_a = ctx.enter_context(tc.psum_pool(name="ps_a", bufs=5))
        ps_l = ctx.enter_context(tc.psum_pool(name="ps_l", bufs=3))
        ctx.enter_context(tc.manual_schedule())

        x_sb = head.tile([P, T * E * J], BF16)
        nc.sync.dma_start(out=x_sb[:], in_=x.rearrange("(p t) e j -> p (t e j)", t=T))
        cal_sb = head.tile([P, E * J], BF16)
        nc.sync.dma_start(out=cal_sb[:], in_=cal.rearrange("e j -> (e j)").partition_broadcast(P))
        tsc = const.tile([P, 4], F32)
        nc.sync.dma_start(out=tsc[:], in_=theta_scale.rearrange("o (p j) z -> p (o j z)", j=4))
        tb = [const.tile([P, 4 * O], U8, name=f"tb{e}") for e in range(E)]

        def load_theta(e):
            nc.sync.dma_start(out=tb[e][:], in_=theta_bytes[e].rearrange("(p j) o -> p (j o)", j=4))

        load_theta(0)
        g_sb = const.tile([P, E * NV], BF16)
        nc.sync.dma_start(out=g_sb[:], in_=g.rearrange("e i -> (e i)").partition_broadcast(P))
        s_bf = head.tile([P, E, 4], BF16)
        nc.sync.dma_start(out=s_bf[:], in_=s.rearrange("(e p t) -> p e t", p=P, t=4))
        for e in range(1, E):
            load_theta(e)
        vs = const.tile([P, E, Q], U8, align_bytes=64)
        vw = const.tile([P, E, 2 * Q], U8, align_bytes=64)
        nc.gpsimd.memset(vs[:].rearrange("p g n -> p (g n)").bitcast(I32), 0)
        nc.sync.dma_start(out=vw[:], in_=v_words.rearrange("g p b -> p g b"))
        for q in range(4):
            nc.sync.dma_start(
                out=vs[32 * q : 32 * q + 4].bitcast(I32),
                in_=v_scales[:, 4 * q : 4 * q + 4, :].rearrange("g r n -> r g n").bitcast(I32),
            )

        warm = head.tile([P, 1], F32)
        nc.vector.memset(warm[:], 0.0)
        warm2 = head.tile([P, 1], F32)
        nc.scalar.activation(out=warm2[:], in_=warm[:], func=ACT.Tanh)
        rn = head.tile([P, T, P], BF16)
        nc.vector.memset(rn[:], 0.0)

        ident = const.tile([P, P], F32)
        make_identity(nc, ident[:])
        ident_b = const.tile([P, P], BF16)
        nc.gpsimd.tensor_copy(out=ident_b[:], in_=ident[:])
        pick2 = head.tile([P, 16], F32)
        nc.gpsimd.tensor_tensor(out=pick2[:], in0=ident[:, 0:16], in1=ident[:, 16:32], op=ALU.add)
        pick = head.tile([P, 16], F32)
        nc.gpsimd.tensor_tensor(out=pick[:], in0=pick2[:], in1=ident[:, 32:48], op=ALU.add)
        gl = const.tile([P, E, 3, P], BF16)
        g_view = g_sb[:].rearrange("p (e m t) -> p e t m", e=E, t=4)

        def make_gl(e):
            for t in range(3):
                c = pick[:, 4 * e + t : 4 * e + t + 1]
                if LG and e > 0:
                    nc.gpsimd.tensor_scalar(out=gl[:, e, t, :], in0=g_view[:, e, t, :], scalar1=c, scalar2=0.0, op0=ALU.mult, op1=ALU.add)
                else:
                    nc.scalar.activation(out=gl[:, e, t, :], in_=g_view[:, e, t, :], func=ACT.Copy, scale=c)

        tw = {}
        tg = {}
        thc = [const.tile([P, O], U32, name=f"thc{e}", align_bytes=64) for e in range(E)]
        ths = [const.tile([P, O], U8, name=f"ths{e}", align_bytes=64) for e in range(E)]

        def theta_widen(e):
            tw[e] = work.tile([P, 4, O], BF16, name="tw", tag="tw", bufs=2)
            for j in range(4):
                nc.scalar.activation(
                    out=tw[e][:, j, :],
                    in_=tb[e][:, j * O : (j + 1) * O].bitcast(FP8),
                    func=ACT.Copy,
                    scale=tsc[:, j : j + 1],
                )

        def theta_interleave(e):
            tg[e] = work.tile([P, 4 * O], BF16, name="tg", tag="tg", bufs=2, align_bytes=64)
            nc.scalar.copy(
                out=tg[e][:].rearrange("p (t m j) -> p m t j", t=4, j=4),
                in_=tw[e][:].rearrange("p j (m t) -> p m t j", t=4),
            )

        def theta_quantize(e):
            nc.vector.quantize_mx(out=thc[e][:].bitcast(FP8X4), scales=ths[e][:], in_=tg[e][:])

        pp = head.tile([P, TE, J, 2], F32)
        dist = head.tile([P, TE * J], F32)
        high = head.tile([P, TE * J], F32)
        bend = head.tile([P, TE * J], F32)
        pv = pp[:].rearrange("p a j b -> p (a j) b")
        q78 = head.tile([P, TE, 4], F32)
        q01 = head.tile([P, TE, 4], F32)
        q23 = head.tile([P, TE, 4], F32)
        q45 = head.tile([P, TE, 4], F32)
        q0123 = head.tile([P, TE, 16], F32)
        qg = head.tile([P, TE, 8], F32)
        w2 = q78[:].rearrange("p (t e) b -> p t (e b)", e=E)
        r1 = head.tile([P, T, 16], F32)
        minus1 = head.tile([P, 1], F32)
        nc.vector.memset(minus1[:], -1.0)
        nc.scalar.activation(out=dist[:], in_=x_sb[:], func=ACT.Abs, scale=2.0, bias=minus1[:])
        nc.scalar.activation(out=high[:], in_=x_sb[:], func=ACT.Relu, scale=2.0, bias=minus1[:])

        def outer(b, dst, u, v, na, nv):
            r = slice(b * TB * E, (b + 1) * TB * E)
            n = TB * E
            nc.vector.tensor_tensor(
                out=dst[:, r, 0 : na * nv].rearrange("p a (b c) -> p a b c", c=nv),
                in0=u[:, r, :].unsqueeze(3).to_broadcast([P, n, na, nv]),
                in1=v[:, r, :].unsqueeze(2).to_broadcast([P, n, na, nv]),
                op=ALU.mult,
            )

        def prepare(b):
            c = slice(b * TB * E * J, (b + 1) * TB * E * J)
            tt = slice(b * TB, (b + 1) * TB)
            V = nc.vector
            return [
                lambda: V.scalar_tensor_tensor(
                    out=bend[:, c].rearrange("p (t c) -> p t c", t=TB),
                    in0=dist[:, c].rearrange("p (t c) -> p t c", t=TB),
                    scalar=-1.0,
                    in1=cal_sb[:].unsqueeze(1).to_broadcast([P, TB, E * J]),
                    op0=ALU.add,
                    op1=ALU.mult,
                ),
                lambda: V.tensor_tensor(out=pv[:, c, 1], in0=high[:, c], in1=bend[:, c], op=ALU.subtract),
                lambda: V.tensor_scalar(out=pv[:, c, 0], in0=pv[:, c, 1], scalar1=-1.0, scalar2=1.0, op0=ALU.mult, op1=ALU.add),
                lambda: outer(b, q78, pp[:, :, 7, :], pp[:, :, 8, :], 2, 2),
                lambda: outer(b, q01, pp[:, :, 0, :], pp[:, :, 1, :], 2, 2),
                lambda: outer(b, q23, pp[:, :, 2, :], pp[:, :, 3, :], 2, 2),
                lambda: V.tensor_copy(out=rn[:, tt, 0:16], in_=w2[:, tt]),
                lambda: outer(b, q45, pp[:, :, 4, :], pp[:, :, 5, :], 2, 2),
                lambda: V.tensor_tensor(out=rn[:, tt, 16:32], in0=w2[:, tt], in1=rn[:, tt, 0:16], op=ALU.subtract),
                lambda: V.tensor_tensor(out=r1[:, tt], in0=w2[:, tt], in1=rn[:, tt, 0:16], op=ALU.subtract),
                lambda: outer(b, q0123, q01[:], q23[:], 4, 4),
                lambda: outer(b, qg, q45[:], pp[:, :, 6, :], 4, 2),
                lambda: V.tensor_tensor(out=rn[:, tt, 32:48], in0=r1[:, tt], in1=rn[:, tt, 16:32], op=ALU.subtract),
            ]

        q0123_v = q0123[:].rearrange("p (t e) b -> p t e b", e=E)
        qg_v = qg[:].rearrange("p (t e) b -> p t e b", e=E)
        q78_v = q78[:].rearrange("p (t e) b -> p t e b", e=E)
        w7 = {}
        y3 = {}
        fs = {}
        gw = {}
        ft = {}
        wg = {}
        wgc = {}
        wgs = {}
        lt = {}
        h = {}
        f = {}
        fc = {}
        fsc = {}
        acc = {}

        gate = {}

        def make_gate(i):
            e, b = i // NB, i % NB
            gate[i] = work.tile([P, TB, 8], F32, name="gate", tag="gate")
            nc.vector.tensor_copy(out=gate[i][:], in_=qg_v[:, TB * b : TB * b + TB, e, :])

        def make_w7(i, eng, src):
            e, b = i // NB, i % NB
            w7[i] = work.tile([P, TB, P], F32, name="w7", tag="w7")
            eng.tensor_tensor(
                out=w7[i][:].rearrange("p t (a b) -> p t a b", b=8),
                in0=q0123_v[:, TB * b : TB * b + TB, e, :].unsqueeze(3).to_broadcast([P, TB, 16, 8]),
                in1=src.unsqueeze(2).to_broadcast([P, TB, 16, 8]),
                op=ALU.mult,
            )

        def make_y3(i, how):
            e, b = i // NB, i % NB
            y3[i] = work.tile([P, TB, P], F32, name="y3", tag="y3")
            if how == "v":
                for k in range(TB):
                    a = (TB * b + k) * E + e
                    nc.vector.tensor_scalar(out=y3[i][:, k, :], in0=g_view[:, e, 3, :], scalar1=q78[:, a, 3:4], scalar2=None, op0=ALU.mult)
            elif how == "s":
                for k in range(TB):
                    a = (TB * b + k) * E + e
                    nc.scalar.activation(out=y3[i][:, k, :], in_=g_view[:, e, 3, :], func=ACT.Copy, scale=q78[:, a, 3:4])
            else:
                nc.gpsimd.tensor_tensor(
                    out=y3[i][:],
                    in0=g_view[:, e, 3, :].unsqueeze(1).to_broadcast([P, TB, P]),
                    in1=gate[i][:, :, 8:9].to_broadcast([P, TB, P]),
                    op=ALU.mult,
                )

        def half_rt(half):
            rt_ps = ps_a.tile([P, TB, P], BF16, name="rt_ps", tag="bank")
            for k in range(TB):
                nc.tensor.transpose(rt_ps[:, k, :], rn[:, TB * half + k, :], ident_b[:])
            nc.scalar.copy(out=rt[:, half * UN : half * UN + UN], in_=rt_ps[:].rearrange("p a n -> p (a n)"))

        def transpose_w7(i):
            ft[i] = ps_a.tile([P, TB, P], F32, name="ft", tag="bank")
            for k in range(TB):
                nc.tensor.transpose(ft[i][:, k, :], w7[i][:, k, :], ident[:])

        def copy_w7(i):
            fs[i] = work.tile([P, TB, P], F32, name="fs", tag="fs")
            nc.scalar.copy(out=fs[i][:], in_=ft[i][:])

        def transpose_y3(i):
            for k in range(TB):
                gw[i, k] = ps_a.tile([P, 4, P], F32, name="gw", tag="bank")
                nc.tensor.transpose(gw[i, k][:, 3, :], y3[i][:, k, :], ident[:])

        def multiply_gw(i):
            e, b = i // NB, i % NB
            for k in range(TB):
                t0 = (TB * b + k) * P
                for t in range(3):
                    nc.tensor.matmul(gw[i, k][:, t, :], lhsT=gl[:, e, t, :], rhs=rt[:, t0 : t0 + P], start=True, stop=True)

        def make_wg(i, k):
            if k == 0:
                wg[i] = work.tile([P, TB, P, 4], BF16, name="wg", tag="wg", align_bytes=64)
            nc.vector.tensor_tensor(
                out=wg[i][:, k],
                in0=gw[i, k][:].rearrange("p t n -> p n t"),
                in1=fs[i][:, k, :].unsqueeze(2).to_broadcast([P, P, 4]),
                op=ALU.mult,
            )

        def quantize_wg(i):
            wgc[i] = work.tile([P, UN], U32, name="wgc", tag="wgc", align_bytes=64)
            wgs[i] = work.tile([P, UN], U8, name="wgs", tag="wgs", align_bytes=64)
            nc.vector.quantize_mx(
                out=wgc[i][:].bitcast(FP8X4), scales=wgs[i][:], in_=wg[i][:].rearrange("p a n t -> p (a n t)")
            )

        def stage1(i, k):
            e = i // NB
            lt[i, k] = ps_l.tile([P, 4, P], F32, name="lt", tag="bank")
            n0 = k * P
            for t in range(4):
                nc.tensor.matmul_mx(
                    out=lt[i, k][:, t, :],
                    lhsT=thc[e][:, t * P : t * P + P].bitcast(FP8X4),
                    lhsT_scale=ths[e][:, t * P : t * P + P],
                    rhs=wgc[i][:, n0 : n0 + P].bitcast(FP8X4),
                    rhs_scale=wgs[i][:, n0 : n0 + P],
                    start=True,
                    stop=True,
                )

        def tanh(i, k):
            if k == 0:
                h[i] = work.tile([P, TB, P, 4], F32, name="h", tag="h")
            nc.scalar.activation(out=h[i][:, k], in_=lt[i, k][:].rearrange("p t n -> p n t"), func=ACT.Tanh)

        def make_f(i, k, n, eng=nc.vector):
            e = i // NB
            if k == 0:
                f[i] = work.tile([P, UN, 4], BF16, name="f", tag="f", align_bytes=64)
            eng.tensor_tensor(
                out=f[i][:, k * P : (k + n) * P, :],
                in0=h[i][:, k : k + n].rearrange("p a n t -> p (a n) t"),
                in1=s_sb[:, e, :].unsqueeze(1).to_broadcast([P, n * P, 4]),
                op=ALU.mult,
            )

        def quantize_f(i, k, n):
            if k == 0:
                fc[i] = const.tile([P, UN], U32, name=f"fc{i}", align_bytes=64)
                fsc[i] = const.tile([P, UN], U8, name=f"fsc{i}", align_bytes=64)
            c = slice(k * P, (k + n) * P)
            nc.vector.quantize_mx(
                out=fc[i][:, c].bitcast(FP8X4), scales=fsc[i][:, c], in_=f[i][:, c, :].rearrange("p n t -> p (n t)")
            )

        def stage2(tile, members):
            b, k = tile // TB, tile % TB
            c = slice(k * P, k * P + P)
            for e in members:
                i = e * NB + b
                nc.tensor.matmul_mx(
                    out=acc[tile][:],
                    lhsT=fc[i][:, c].bitcast(FP8X4),
                    lhsT_scale=fsc[i][:, c],
                    rhs=vw[:, e, :].bitcast(FP4X4),
                    rhs_scale=vs[:, e, :],
                    start=(e == 0),
                    stop=(e == E - 1),
                )

        out_v = out.rearrange("(p t) q -> t p q", t=T)

        def store(tile, on_vector):
            o = work.tile([P, Q], F32, name="o", tag="o", bufs=8)
            if on_vector:
                nc.vector.tensor_copy(out=o[:], in_=acc[tile][:])
            else:
                nc.scalar.copy(out=o[:], in_=acc[tile][:])
            nc.sync.dma_start(out=out_v[tile], in_=o[:])

        rt = const.tile([P, N], BF16)
        s_sb = const.tile([P, E, 4], F32)
        nc.gpsimd.tensor_copy(out=s_sb[:], in_=s_bf[:])
        theta_widen(0)
        make_gl(0)
        for step in prepare(0):
            step()
        make_w7(0, nc.vector, qg_v[:, 0:TB, 0, 0:8])
        half_rt(0)
        make_y3(0, "s")
        transpose_w7(0)
        copy_w7(0)
        transpose_y3(0)
        multiply_gw(0)
        rest = prepare(1)
        weave = [6, 9, 11, 13]
        for k in range(TB):
            for n in range(weave[k - 1] if k else 0, weave[k]):
                rest[n]()
            make_wg(0, k)
        theta_interleave(0)
        half_rt(1)
        make_y3(1, "s")
        make_w7(1, nc.vector, qg_v[:, TB:T, 0, 0:8])
        transpose_w7(1)
        copy_w7(1)
        theta_quantize(0)

        for i in range(UNITS):
            if i + 2 < UNITS:
                make_gate(i + 2)
                make_w7(i + 2, nc.gpsimd, gate[i + 2][:, :, 0:8])
            if i % NB == 0 and i // NB + 1 < E and LG:
                make_gl(i // NB + 1)
            if FG and i >= 2:
                make_f(i - 2, 3, 1, nc.gpsimd)
            if i > 0:
                for k in range(TB):
                    make_wg(i, k)
            if i >= 2:
                quantize_f(i - 2, 0, TB)
            if i % NB == 0 and i > 0:
                theta_quantize(i // NB)
            if i + 2 < UNITS:
                make_y3(i + 2, Y3)
            if i % NB == 0 and i // NB + 1 < E:
                if not LG:
                    make_gl(i // NB + 1)
                theta_widen(i // NB + 1)
            if i % NB == 1 and i // NB + 1 < E:
                theta_interleave(i // NB + 1)
            if i + 1 < UNITS:
                transpose_y3(i + 1)
                multiply_gw(i + 1)
            if i == UNITS - 1:
                quantize_wg(i)
                make_f(i - 1, 0, 4)
            else:
                if i >= 1:
                    make_f(i - 1, 0, 2)
                quantize_wg(i)
                if i >= 1:
                    make_f(i - 1, 2, 1 if FG else 2)
            if i == UNITS - 1:
                for tile in range(TB):
                    acc[tile] = ps_a.tile([P, Q], F32, name="acc", tag="bank")
                    stage2(tile, range(E - 1))
            for k in range(TB):
                stage1(i, k)
                tanh(i, k)
            if i + 2 < UNITS:
                transpose_w7(i + 2)
                copy_w7(i + 2)

        last = UNITS - 1
        acc[TB] = ps_a.tile([P, Q], F32, name="acc", tag="bank")
        stage2(TB, range(E - 1))
        quantize_f(last - 1, 0, TB)
        for tile in range(TB + 1, T):
            acc[tile] = ps_l.tile([P, Q], F32, name="acc2", tag="bank")
            stage2(tile, range(E - 1))
        for tile in range(TB):
            stage2(tile, [E - 1])
            store(tile, False)
        for k in range(TB):
            make_f(last, k, 1)
            if k % 2 == 1:
                quantize_f(last, k - 1, 2)
        for tile in range(TB, T):
            stage2(tile, [E - 1])
            store(tile, tile >= T - 2)
